import numpy as np
import ml_dtypes

BF16 = ml_dtypes.bfloat16


def bf(x):
    return np.asarray(x, np.float32).astype(BF16)


def f32(x):
    return np.asarray(x, np.float32)


def f64(x):
    return np.asarray(x).astype(np.float64)


def striped(idx):
    return np.tile(idx.reshape(-1, 16).T, (8, 1))


def rows(idx, k):
    return np.tile(idx, (k, 1))


def look(tab, idx):
    return np.take_along_axis(f64(tab), rows(idx, len(tab)), axis=1)


K, S, V, N, M = 256, 256, 256, 256, 128


def setup_inputs():
    return {"tab": f32(np.random.standard_normal((K, S))), "y": f32(np.random.standard_normal((K, V))), "w": bf(np.random.standard_normal((K, M)) / np.sqrt(K)), "offs": striped(np.random.permutation(S)[:N])}


def reference(tab, y, w, offs):
    idx = offs[:16].T.reshape(-1)
    t = look(tab, idx)
    x = 1.0 / (1.0 + np.exp(-t)) * f64(y)
    y = f64(w).T @ x
    return y

@@ -1,0 +1,50 @@
+import concourse.mybir as mybir
+
+P = 128
+ROWS, COLS, M = 256, 256, 128
+BLOCKS = ROWS // P
+HALVES = 2
+HALF = COLS // HALVES
+ENTRIES_PER_COLUMN = 16
+FLOPS = 2 * ROWS * COLS * M
+
+F32, BF16, U16 = mybir.dt.float32, mybir.dt.bfloat16, mybir.dt.uint16
+SIGMOID = mybir.ActivationFunctionType.Sigmoid
+MULT = mybir.AluOpType.mult
+
+
+def tile_lookup_gate_sig_none_kernel(tc, tab, y, w, offs, out):
+    nc = tc.nc
+    tab_rows = tab.rearrange("(p b) s -> p b s", b=BLOCKS)
+    y_rows = y.rearrange("(p b) j -> p b j", b=BLOCKS)
+    w_rows = w.rearrange("(p b) m -> p b m", b=BLOCKS)
+
+    with (
+        tc.tile_pool(name="held", bufs=1) as held,
+        tc.psum_pool(name="psum", bufs=1) as psum,
+    ):
+        offsets = held.tile([P, COLS // ENTRIES_PER_COLUMN], U16, name="offsets")
+        windows = [held.tile([P, COLS], F32, name=f"window{b}") for b in range(BLOCKS)]
+        stream = held.tile([P, BLOCKS, COLS], F32, name="stream")
+        weights = held.tile([P, BLOCKS, M], BF16, name="weights")
+
+        nc.sync.dma_start(offsets[:], offs)
+        for b in range(BLOCKS):
+            nc.sync.dma_start(windows[b][:], tab_rows[:, b, :])
+        nc.sync.dma_start(stream[:], y_rows)
+        nc.sync.dma_start(weights[:], w_rows)
+
+        list_columns = HALF // ENTRIES_PER_COLUMN
+        for h in range(HALVES):
+            cols = slice(h * HALF, (h + 1) * HALF)
+            half_list = offsets[:, h * list_columns : (h + 1) * list_columns]
+            acc = psum.tile([P, HALF], F32, name=f"acc{h}")
+            for b in range(BLOCKS):
+                gate = held.tile([P, HALF], F32, name=f"gate{h}{b}")
+                x = held.tile([P, HALF], BF16, name=f"x{h}{b}")
+                nc.scalar.activation(gate[:], windows[b][:].indirect(half_list), SIGMOID)
+                nc.vector.tensor_tensor(x[:], gate[:], stream[:, b, cols], MULT)
+                nc.tensor.matmul(acc[:], weights[:, b, :], x[:], start=(b == 0), stop=(b == BLOCKS - 1))
+            result = held.tile([P, HALF], F32, name=f"result{h}")
+            nc.vector.tensor_copy(result[:], acc[:])
+            nc.sync.dma_start(out[:, cols], result[:])

@@ -28,6 +28,11 @@ def tile_lookup_gate_sig_none_kernel(tc, tab, y, w, offs, out):
         stream = held.tile([P, BLOCKS, COLS], F32, name="stream")
         weights = held.tile([P, BLOCKS, M], BF16, name="weights")
 
+        warm_in = held.tile([P, 1], F32, name="warm_in")
+        warm_out = held.tile([P, 1], F32, name="warm_out")
+        nc.vector.memset(warm_in[:], 0.0)
+        nc.scalar.activation(warm_out[:], warm_in[:], SIGMOID)
+
         nc.sync.dma_start(offsets[:], offs)
         for b in range(BLOCKS):
             nc.sync.dma_start(windows[b][:], tab_rows[:, b, :])

@@ -5,6 +5,7 @@ ROWS, COLS, M = 256, 256, 128
 BLOCKS = ROWS // P
 HALVES = 2
 HALF = COLS // HALVES
+PIECES = ((0, HALF), (HALF, HALF // 2), (HALF + HALF // 2, HALF // 2))
 ENTRIES_PER_COLUMN = 16
 FLOPS = 2 * ROWS * COLS * M
 
@@ -25,31 +26,35 @@ def tile_lookup_gate_sig_none_kernel(tc, tab, y, w, offs, out):
     ):
         offsets = held.tile([P, COLS // ENTRIES_PER_COLUMN], U16, name="offsets")
         windows = [held.tile([P, COLS], F32, name=f"window{b}") for b in range(BLOCKS)]
-        stream = held.tile([P, BLOCKS, COLS], F32, name="stream")
+        streams = [held.tile([P, COLS], F32, name=f"stream{b}") for b in range(BLOCKS)]
         weights = held.tile([P, BLOCKS, M], BF16, name="weights")
+
+        nc.scalar.dma_start(windows[0][:], tab_rows[:, 0, :])
+        nc.sync.dma_start(offsets[:], offs)
 
         warm_in = held.tile([P, 1], F32, name="warm_in")
         warm_out = held.tile([P, 1], F32, name="warm_out")
         nc.vector.memset(warm_in[:], 0.0)
         nc.scalar.activation(warm_out[:], warm_in[:], SIGMOID)
 
-        nc.sync.dma_start(offsets[:], offs)
-        for b in range(BLOCKS):
-            nc.sync.dma_start(windows[b][:], tab_rows[:, b, :])
-        nc.sync.dma_start(stream[:], y_rows)
+        nc.sync.dma_start(windows[1][:], tab_rows[:, 1, :])
+        nc.sync.dma_start(streams[0][:], y_rows[:, 0, :])
         nc.sync.dma_start(weights[:], w_rows)
+        nc.sync.dma_start(streams[1][:], y_rows[:, 1, :])
 
-        list_columns = HALF // ENTRIES_PER_COLUMN
+        accs = [psum.tile([P, width], F32, name=f"acc{first}") for first, width in PIECES]
+        for b in range(BLOCKS):
+            for acc, (first, width) in zip(accs, PIECES):
+                entries = offsets[:, first // ENTRIES_PER_COLUMN : (first + width) // ENTRIES_PER_COLUMN]
+                gate = held.tile([P, width], F32, name=f"gate{b}_{first}")
+                x = held.tile([P, width], BF16, name=f"x{b}_{first}")
+                nc.scalar.activation(gate[:], windows[b][:].indirect(entries), SIGMOID)
+                nc.vector.tensor_tensor(x[:], gate[:], streams[b][:, first : first + width], MULT)
+                nc.tensor.matmul(acc[:], weights[:, b, :], x[:], start=(b == 0), stop=(b == BLOCKS - 1))
+
+        result = held.tile([P, COLS], F32, name="result")
+        for acc, (first, width) in zip(accs, PIECES):
+            nc.vector.tensor_copy(result[:, first : first + width], acc[:])
         for h in range(HALVES):
             cols = slice(h * HALF, (h + 1) * HALF)
-            half_list = offsets[:, h * list_columns : (h + 1) * list_columns]
-            acc = psum.tile([P, HALF], F32, name=f"acc{h}")
-            for b in range(BLOCKS):
-                gate = held.tile([P, HALF], F32, name=f"gate{h}{b}")
-                x = held.tile([P, HALF], BF16, name=f"x{h}{b}")
-                nc.scalar.activation(gate[:], windows[b][:].indirect(half_list), SIGMOID)
-                nc.vector.tensor_tensor(x[:], gate[:], stream[:, b, cols], MULT)
-                nc.tensor.matmul(acc[:], weights[:, b, :], x[:], start=(b == 0), stop=(b == BLOCKS - 1))
-            result = held.tile([P, HALF], F32, name=f"result{h}")
-            nc.vector.tensor_copy(result[:], acc[:])
-            nc.sync.dma_start(out[:, cols], result[:])
+            nc.sync.dma_start(out[:, cols], result[:, cols])

@@ -29,14 +29,13 @@ def tile_lookup_gate_sig_none_kernel(tc, tab, y, w, offs, out):
         streams = [held.tile([P, COLS], F32, name=f"stream{b}") for b in range(BLOCKS)]
         weights = held.tile([P, BLOCKS, M], BF16, name="weights")
 
-        nc.scalar.dma_start(windows[0][:], tab_rows[:, 0, :])
-        nc.sync.dma_start(offsets[:], offs)
-
         warm_in = held.tile([P, 1], F32, name="warm_in")
         warm_out = held.tile([P, 1], F32, name="warm_out")
         nc.vector.memset(warm_in[:], 0.0)
         nc.scalar.activation(warm_out[:], warm_in[:], SIGMOID)
 
+        nc.sync.dma_start(windows[0][:], tab_rows[:, 0, :])
+        nc.sync.dma_start(offsets[:], offs)
         nc.sync.dma_start(windows[1][:], tab_rows[:, 1, :])
         nc.sync.dma_start(streams[0][:], y_rows[:, 0, :])
         nc.sync.dma_start(weights[:], w_rows)

@@ -38,8 +38,8 @@ def tile_lookup_gate_sig_none_kernel(tc, tab, y, w, offs, out):
         nc.sync.dma_start(offsets[:], offs)
         nc.sync.dma_start(windows[1][:], tab_rows[:, 1, :])
         nc.sync.dma_start(streams[0][:], y_rows[:, 0, :])
-        nc.sync.dma_start(weights[:], w_rows)
         nc.sync.dma_start(streams[1][:], y_rows[:, 1, :])
+        nc.sync.dma_start(weights[:], w_rows)
 
         accs = [psum.tile([P, width], F32, name=f"acc{first}") for first, width in PIECES]
         for b in range(BLOCKS):

import concourse.mybir as mybir

P = 128
ROWS, COLS, M = 256, 256, 128
BLOCKS = ROWS // P
HALVES = 2
HALF = COLS // HALVES
PIECES = ((0, HALF), (HALF, HALF // 2), (HALF + HALF // 2, HALF // 2))
ENTRIES_PER_COLUMN = 16
FLOPS = 2 * ROWS * COLS * M

F32, BF16, U16 = mybir.dt.float32, mybir.dt.bfloat16, mybir.dt.uint16
SIGMOID = mybir.ActivationFunctionType.Sigmoid
MULT = mybir.AluOpType.mult


def tile_lookup_gate_sig_none_kernel(tc, tab, y, w, offs, out):
    nc = tc.nc
    tab_rows = tab.rearrange("(p b) s -> p b s", b=BLOCKS)
    y_rows = y.rearrange("(p b) j -> p b j", b=BLOCKS)
    w_rows = w.rearrange("(p b) m -> p b m", b=BLOCKS)

    with (
        tc.tile_pool(name="held", bufs=1) as held,
        tc.psum_pool(name="psum", bufs=1) as psum,
    ):
        offsets = held.tile([P, COLS // ENTRIES_PER_COLUMN], U16, name="offsets")
        windows = [held.tile([P, COLS], F32, name=f"window{b}") for b in range(BLOCKS)]
        streams = [held.tile([P, COLS], F32, name=f"stream{b}") for b in range(BLOCKS)]
        weights = held.tile([P, BLOCKS, M], BF16, name="weights")

        warm_in = held.tile([P, 1], F32, name="warm_in")
        warm_out = held.tile([P, 1], F32, name="warm_out")
        nc.vector.memset(warm_in[:], 0.0)
        nc.scalar.activation(warm_out[:], warm_in[:], SIGMOID)

        nc.sync.dma_start(windows[0][:], tab_rows[:, 0, :])
        nc.sync.dma_start(offsets[:], offs)
        nc.sync.dma_start(windows[1][:], tab_rows[:, 1, :])
        nc.sync.dma_start(streams[0][:], y_rows[:, 0, :])
        nc.sync.dma_start(streams[1][:], y_rows[:, 1, :])
        nc.sync.dma_start(weights[:], w_rows)

        accs = [psum.tile([P, width], F32, name=f"acc{first}") for first, width in PIECES]
        for b in range(BLOCKS):
            for acc, (first, width) in zip(accs, PIECES):
                entries = offsets[:, first // ENTRIES_PER_COLUMN : (first + width) // ENTRIES_PER_COLUMN]
                gate = held.tile([P, width], F32, name=f"gate{b}_{first}")
                x = held.tile([P, width], BF16, name=f"x{b}_{first}")
                nc.scalar.activation(gate[:], windows[b][:].indirect(entries), SIGMOID)
                nc.vector.tensor_tensor(x[:], gate[:], streams[b][:, first : first + width], MULT)
                nc.tensor.matmul(acc[:], weights[:, b, :], x[:], start=(b == 0), stop=(b == BLOCKS - 1))

        result = held.tile([P, COLS], F32, name="result")
        for acc, (first, width) in zip(accs, PIECES):
            nc.vector.tensor_copy(result[:, first : first + width], acc[:])
        for h in range(HALVES):
            cols = slice(h * HALF, (h + 1) * HALF)
            nc.sync.dma_start(out[:, cols], result[:, cols])
